import numpy as np, ml_dtypes
CORES = [23,119,17,113]
N = 4
import mx_ref
BF = ml_dtypes.bfloat16
def entries(a):
    return np.ascontiguousarray(a.T).reshape(-1)
def table(e):
    return np.ascontiguousarray(np.reshape(e, (-1, 16)).T).astype(np.int32)
def tile(rs):
    return np.stack(rs, axis=2).reshape(128, -1).astype(BF)
def cut(t, i, w=512):
    return t[:, w * i:w * i + w]
def f(rng, *shape):
    return mx_ref.flush((rng.standard_normal(shape, dtype=np.float32) * np.exp2(rng.integers(-2, 3, shape[:-1] + (1,)))).astype(BF))
def wide(rng, *shape, cols=0):
    v = rng.standard_normal(shape, dtype=np.float32) * np.exp2(rng.integers(-12, 13, shape)).astype(np.float32)
    if cols: v *= np.repeat(np.exp2(rng.integers(-cols, cols + 1, shape[:-2] + (1, shape[-1] // 4))) * (rng.random(shape[:-2] + (1, shape[-1] // 4)) > 0.0625), 4, axis=-1).astype(np.float32)
    return mx_ref.flush(v.astype(BF))
T, TG, C1, C2 = 512, 256, 320, 64
def layer(rng, C, M, own=0.25, full=False, hub=False, neg=None):
    snd = np.full((N, N, C), -1); src = np.zeros((N, M, 4), int)
    for s in range(N):
        for r in range(N):
            if s != r and own < 1:
                n = C if full else rng.integers(1, C + 1)
                snd[s, r, rng.permutation(C)[:n]] = rng.choice(T, n, replace=False)
    h, k, c = rng.integers(0, N), rng.integers(0, T), rng.integers(0, C, N)
    if hub:
        for r in range(N):
            if r != h: snd[h, r, c[r]] = k
    for r in range(N):
        src[r] = rng.integers(0, T, (M, 4))
        if own < 1:
            far = T + np.flatnonzero(snd[:, r].reshape(-1) >= 0)
            src[r] = np.where(rng.random((M, 4)) < own, src[r], rng.choice(far, (M, 4)))
        if hub:
            e = k if r == h else T + h * C + c[r]
            src[r][:, 0] = e; src[r][rng.permutation(M)[:M // 4]] = e
            src[r] = rng.permuted(src[r], axis=1)
        if neg is not None:
            bad = np.flatnonzero(np.concatenate([neg[r]] + [(snd[s, r] >= 0) & neg[s][snd[s, r]] for s in range(N)]))
            src[r][rng.permutation(M)[:M // 2]] = rng.choice(bad, (M // 2, 4))
    return np.stack([table(a) for a in snd]), np.stack([table(a) for a in src])
def lists(rng, neg=None, **o):
    a, b = layer(rng, C1, T, neg=neg, **o); c, e = layer(rng, C2, TG, **o)
    return {"snd1": a, "src1": b, "snd2": c, "src2": e}
def setup_inputs(rng):
    return {"x": f(rng, N, 128, 4 * T), "w1": np.repeat(f(rng, 1, 128, 4 * 512), N, axis=0), "w2": np.repeat(f(rng, 1, 128, 512), N, axis=0), **lists(rng)}
def setup_inputs_foreign(rng):
    return {**setup_inputs(rng), **lists(rng, own=0, full=True)}
def setup_inputs_hub(rng):
    return {**setup_inputs(rng), **lists(rng, hub=True)}
def setup_inputs_negative(rng):
    d = setup_inputs(rng)
    neg = np.stack([rng.permutation(T) < T // 2 for r in range(N)])
    v = np.abs(d["x"]).reshape(N, 128, T, 4)
    d["x"] = np.where(neg[:, None, :, None], -v, v).reshape(N, 128, 4 * T)
    d["w1"] = np.abs(d["w1"])
    return {**d, **lists(rng, neg=neg)}
def setup_inputs_self(rng):
    return {**setup_inputs(rng), **lists(rng, own=1)}
def setup_inputs_spread(rng):
    d = setup_inputs(rng); d["x"] = wide(rng, N, 128, 4 * T); return d
def check_inputs(d):
    b = []
    for k in ("w1", "w2"):
        if any(d[k][r].tobytes() != d[k][0].tobytes() for r in range(N)): b.append(k)
    for l, C in (("1", C1), ("2", C2)):
        snd = np.stack([entries(a) for a in d["snd" + l]]).reshape(N, N, C)
        if snd.min() < -1 or snd.max() >= T: b.append("snd" + l)
        for r in range(N):
            if (snd[r, r] != -1).any(): b.append("snd" + l)
            ok = np.concatenate([np.ones(T, bool), snd[:, r].reshape(-1) >= 0])
            e = entries(d["src" + l][r])
            if e.min() < 0 or e.max() >= T + N * C or not ok[e].all(): b.append("src" + l)
    return b
def most(v, snd, src, r, C):
    a = np.concatenate([v[r]] + [v[s][:, entries(snd[s])[r * C:r * C + C]] for s in range(N)], axis=1)
    return a[:, entries(src[r])].reshape(128, -1, 4).max(axis=2)
def reference(x, w1, w2, snd1, src1, snd2, src2):
    q = [mx_ref.quantize(x[r]) for r in range(N)]
    Z = [[mx_ref.matmul(mx_ref.quantize(cut(w1[r], i)), q[r]) for r in range(N)] for i in range(4)]
    U = []
    for r in range(N):
        h = tile([np.maximum(most(Z[i], snd1, src1, r, C1), np.float32(0)) * np.float32(0.05) for i in range(4)])
        U.append(mx_ref.matmul(mx_ref.quantize(w2[r]), mx_ref.quantize(h)))
    return {"y": np.stack([most(U, snd2, src2, r, C2) for r in range(N)])}

import numpy as np
from concourse.bass import DstId, RemoteDMATransfer, IndirectOffsetOnAxis
from concourse.mybir import dt, AluOpType, ActivationFunctionType

N, NODES, TG, C1, C2 = 4, 512, 256, 320, 64
W1T = NODES + N * C1
W2T = NODES + N * C2
F8 = "float8_e4m3fn_x4"
SCRATCH = {
    "xb": ("sbuf", [128, 2048], "bfloat16"), "xq": ("sbuf", [128, 512], F8), "xp": ("sbuf", [128, 512], "uint8"),
    "w1b": ("sbuf", [128, 2048], "bfloat16"), "w1q": ("sbuf", [128, 512], F8), "w1p": ("sbuf", [128, 512], "uint8"),
    "w2b": ("sbuf", [128, 512], "bfloat16"), "w2q": ("sbuf", [128, 128], F8), "w2p": ("sbuf", [128, 128], "uint8"),
    "xs": ("sbuf", [128, 12 * C1], "bfloat16"), "xsq": ("sbuf", [128, 3 * C1], F8), "xsp": ("sbuf", [128, 3 * C1], "uint8"),
    "c1": ("sbuf", [128, 3 * C1], F8), "p1": ("sbuf", [128, 3 * C1], "uint8"),
    "r0": ("sbuf", [128, W1T], "bfloat16"), "r1": ("sbuf", [128, W1T], "bfloat16"),
    "r2": ("sbuf", [128, W1T], "bfloat16"), "r3": ("sbuf", [128, W1T], "bfloat16"),
    "h": ("sbuf", [128, 2048], "bfloat16"), "hq": ("sbuf", [128, 512], F8), "hp": ("sbuf", [128, 512], "uint8"),
    "hs": ("sbuf", [128, 12 * C2], "bfloat16"), "hsq": ("sbuf", [128, 3 * C2], F8), "hsp": ("sbuf", [128, 3 * C2], "uint8"),
    "c2": ("sbuf", [128, 3 * C2], F8), "p2": ("sbuf", [128, 3 * C2], "uint8"),
    "mask": ("sbuf", [128, 1536], "bfloat16"),
    "bs": ("sbuf", [128, 4 * 576], "bfloat16"), "bt": ("sbuf", [128, 4 * 576], "bfloat16"),
    "bh": ("sbuf", [128, 2 * 1536], "bfloat16"), "bi": ("sbuf", [128, 2 * 1536], "bfloat16"),
    "u": ("sbuf", [128, W2T], "float32"), "yb": ("sbuf", [128, TG], "float32"),
    "sl": ("sbuf", [128, 80], "int32"), "sl4": ("sbuf", [128, 80], "int32"), "so": ("sbuf", [128, 320], "uint16"),
    "l1": ("sbuf", [16, 128], "int32"), "lc1": ("sbuf", [16, 128], "int32"), "d1": ("dram", [16, 128], "int32"),
    "e1": ("sbuf", [128, 128], "int32"), "o1": ("sbuf", [128, 128], "uint16"),
    "l2": ("sbuf", [16, 64], "int32"), "lc2": ("sbuf", [16, 64], "int32"), "d2": ("dram", [16, 64], "int32"),
    "e2": ("sbuf", [128, 64], "int32"), "o2": ("sbuf", [128, 64], "uint16"),
    "li": ("sbuf", [32, 64], "int32"), "lf": ("sbuf", [32, 64], "float32"), "lt": ("sbuf", [32, 64], "float32"),
    "t4": ("dram", [512, 4], "float32"),
    "dsn": ("dram", [16, 12], "int32"), "ix": ("sbuf", [128, 2], "int32"), "ixc": ("sbuf", [128, 2], "int32"),
    "cr": ("sbuf", [128, 8], "float32"), "ec": ("sbuf", [128, 48], "float32"), "oc": ("sbuf", [128, 48], "uint16"),
    "ps": ("psum", [128, 4096], "float32"),
}
SEMAPHORES = ["cv", "cs", "ct", "d_snd", "d_x", "g_l", "d_dsn", "d_ix", "d_l2", "d_w1", "d_w2", "d_t4", "d_d1", "d_e1",
              "d_d2", "d_e2", "g_i", "d_ec", "d_y", "a1_0", "a1_1", "a1_2", "a2", "sent"]


def rank_program(g, core, T, topo):
    r = T.rank_of(core)
    if r is None:
        return
    V, S, P, Y = g.vector, g.scalar, g.tensor, g.sync
    queues = {"g": g, "V": V, "S": S, "P": P, "Y": Y}
    MAX, MULT, ADD = AluOpType.max, AluOpType.mult, AluOpType.add
    COPY, RELU = ActivationFunctionType.Copy, ActivationFunctionType.Relu
    U8 = dt.uint8
    count = {}
    seen = {}

    def done(sem, ins, k=1):
        ins.then_inc(T.sem[sem], k)
        count[sem] = count.get(sem, 0) + k
        return (sem, count[sem])

    def need(q, *toks):
        for sem, k in toks:
            if seen.get((q, sem), 0) < k:
                queues[q].wait_ge(T.sem[sem], k)
                seen[(q, sem)] = k

    def v(ins): return done("cv", ins)
    def s(ins): return done("cs", ins)
    def p(ins): return done("ct", ins)
    def dma(sem, ins): return done(sem, ins, 16)

    others = [d for d in range(N) if d != r]
    me = T.cores[r]
    far = [d for d in others if topo.chip(T.cores[d]) != topo.chip(me)]
    far.sort(key=lambda d: topo.die(T.cores[d]) != topo.die(me))
    near = [d for d in others if d not in far]
    order = [far[0], far[1], near[0]]
    arrive = [far[0], near[0], far[1]]
    far_eng = topo.engines(me, T.cores[far[0]])
    near_eng = [e for e in topo.engines(me, T.cores[near[0]]) if e not in far_eng]
    half = len(far_eng) // 2

    def bits(es): return sum(1 << e for e in es)
    def slot(a, b): return a - (1 if a > b else 0)
    runs = []
    for d in others:
        if runs and runs[-1][0] + runs[-1][1] == d: runs[-1][1] += 1
        else: runs.append([d, 1])

    for k in range(4):
        dma("d_snd", Y.dma_start(out=T.sl[16 * k:16 * k + 16, :], in_=T.snd1[:, :]))
        t_snd = dma("d_snd", S.dma_start(out=T.sl[16 * (k + 4):16 * (k + 4) + 16, :], in_=T.snd1[:, :]))
    dma("d_x", Y.dma_start(out=T.xb[:, 0:1024], in_=T.x[:, 0:1024]))
    t_x = dma("d_x", S.dma_start(out=T.xb[:, 1024:2048], in_=T.x[:, 1024:2048]))
    for k in range(2):
        dma("g_l", g.dma_start(out=T.li[16 * k:16 * k + 16, :], in_=T.src1[:, 64 * k:64 * k + 64]))
    t_l = dma("g_l", g.dma_start(out=T.l1[:, :], in_=T.src1[:, :]))
    c = 0
    for d, n in runs:
        t_dsn = dma("d_dsn", Y.dma_start(out=T.dsn[:, c:c + 4 * n], in_=T.snd2[:, 4 * d:4 * d + 4 * n]))
        c += 4 * n
    dma("d_w1", Y.dma_start(out=T.w1b[:, 0:1024], in_=T.w1[:, 0:1024]))
    t_w1 = dma("d_w1", S.dma_start(out=T.w1b[:, 1024:2048], in_=T.w1[:, 1024:2048]))
    t_l2 = dma("d_l2", Y.dma_start(out=T.l2[:, :], in_=T.src2[:, :]))
    t_w2 = dma("d_w2", Y.dma_start(out=T.w2b[:, :], in_=T.w2[:, :]))
    need("Y", t_dsn)
    t_ix = dma("d_ix", Y.dma_start(out=T.ix[0:96, :], in_=T.dsn[:, :]))

    R = [T["r%d" % i] for i in range(4)]
    t_one = v(V.memset(T.mask[:, :], 1.0))
    for i in range(4):
        t_r = v(V.memset(R[i][:, NODES + C1 * r:NODES + C1 * r + C1], 0.0))
    t_u = v(V.memset(T.u[:, NODES + C2 * r:NODES + C2 * r + C2], 0.0))
    need("V", t_one)
    t_mask = v(V.memset(T.mask[:, 0::3], 0.0))

    need("V", t_snd)
    t_a = v(V.tensor_scalar(out=T.sl4[:, :], in0=T.sl[:, :], scalar1=0.0, scalar2=4.0, op0=MAX, op1=MULT))
    need("V", t_a)
    for t in range(4):
        t_so = v(V.tensor_scalar(out=T.so[:, 80 * t:80 * t + 80], in0=T.sl4[:, :], scalar1=float(t), scalar2=None, op0=ADD))

    def listed(j, t):
        d = order[j]
        return (T.xs[:, 4 * C1 * j + t:4 * C1 * (j + 1):4], T.xb[:, 0:2048].indirect(T.so[:, 80 * t + 20 * d:80 * t + 20 * d + 20]))

    def to(d):
        rid, pid, _ = topo.addr(T.cores[d])
        return rid, pid

    def send1(kind, j):
        d = order[j]
        k = slot(r, d)
        rid, pid = to(d)
        a, b = (T.c1, T.xsq) if kind == "codes" else (T.p1, T.xsp)
        o, i = a[:, C1 * k:C1 * k + C1], b[:, C1 * j:C1 * j + C1]
        if kind == "codes": o, i = o.bitcast(U8), i.bitcast(U8)
        es = near_eng if d in near else far_eng
        g.remote_dma(o, i, T.sem["a1_%d" % k], T.sem.sent, pid, rid, bits(es))
        count["sent"] = count.get("sent", 0) + len(es)

    def fused(pairs, sem_of, engs):
        ts = []
        for (o, i, d), sm, es in zip(pairs, sem_of, engs):
            rid, pid = to(d)
            ts.append(RemoteDMATransfer(dst_ids=[DstId(rid=rid, pnc=pid)], dma_engine_mask=bits(es), remote_sem=T.sem[sm], src=i, dst=o))
            count["sent"] = count.get("sent", 0) + len(es)
        g.remote_dma_fused(ts, local_sem=T.sem.sent)

    need("V", t_x, t_so)
    need("S", t_x, t_so)
    t_q = []
    for j in range(3):
        for t in (0, 1):
            o, i = listed(j, t)
            t_v = v(V.tensor_copy(out=o, in_=i))
        for t in (2, 3):
            o, i = listed(j, t)
            t_s = s(S.activation(out=o, in_=i, func=COPY))
        need("V", t_s, t_v)
        t_q.append(v(V.quantize_mx(out=T.xsq[:, C1 * j:C1 * j + C1], scales=T.xsp[:, C1 * j:C1 * j + C1], in_=T.xs[:, 4 * C1 * j:4 * C1 * j + 4 * C1])))
        if j == 0:
            need("V", t_l)
            t_a = v(V.tensor_copy(out=T.lf[:, :], in_=T.li[:, :]))
            for q in range(4):
                t_lc1 = v(V.tensor_copy(out=T.lc1[:, 32 * q:32 * q + 32], in_=T.l1[:, q:128:4]))
            need("V", t_a)
            t_lt = v(V.transpose(out=T.lt[:, :], in_=T.lf[:, :]))
            need("V", t_ix)
            t_ixc = v(V.tensor_scalar(out=T.ixc[0:96, :], in0=T.ix[0:96, :], scalar1=0.0, scalar2=None, op0=MAX))
    need("g", t_q[0])
    send1("codes", 0)
    send1("planes", 0)
    need("g", t_q[1])
    send1("codes", 1)
    need("g", t_q[2])
    send1("codes", 2)
    fused([(T.p1[:, C1 * slot(r, order[j]):C1 * slot(r, order[j]) + C1], T.xsp[:, C1 * j:C1 * j + C1], order[j]) for j in (1, 2)],
          ["a1_%d" % slot(r, order[j]) for j in (1, 2)], [far_eng, near_eng])

    need("Y", t_lt)
    for hh in range(2):
        for b in range(2):
            n0 = 256 * hh + 128 * b
            t_t4 = dma("d_t4", Y.dma_start(out=T.t4[n0:n0 + 128, :], in_=T.lt[:, 32 * b + 16 * hh:32 * b + 16 * hh + 16]))
    need("Y", t_lc1)
    for q in range(4):
        t_d1 = dma("d_d1", Y.dma_start(out=T.d1[4 * q:4 * q + 4, :], in_=T.lc1[:, 32 * q:32 * q + 32]))
    need("Y", t_d1)
    for k in range(8):
        t_e1 = dma("d_e1", Y.dma_start(out=T.e1[16 * k:16 * k + 16, :], in_=T.d1[:, :]))
    need("g", t_t4, t_ixc)
    for k in range(2):
        t_i = dma("g_i", g.indirect_dma_start(out=T.cr[0:96, 4 * k:4 * k + 4], out_offset=None, in_=T.t4[:],
                                              in_offset=IndirectOffsetOnAxis(ap=T.ixc[0:96, k:k + 1], axis=0), bounds_check=NODES - 1))

    need("V", t_w1)
    t_wq = v(V.quantize_mx(out=T.w1q[:, :], scales=T.w1p[:, :], in_=T.w1b[:, :]))
    t_xq = v(V.quantize_mx(out=T.xq[:, :], scales=T.xp[:, :], in_=T.xb[:, :]))
    need("V", t_l2)
    for q in range(4):
        t_lc2 = v(V.tensor_copy(out=T.lc2[:, 16 * q:16 * q + 16], in_=T.l2[:, q:64:4]))
    need("V", t_w2)
    t_w2q = v(V.quantize_mx(out=T.w2q[:, :], scales=T.w2p[:, :], in_=T.w2b[:, :]))
    need("Y", t_lc2)
    for q in range(4):
        t_d2 = dma("d_d2", Y.dma_start(out=T.d2[4 * q:4 * q + 4, :], in_=T.lc2[:, 16 * q:16 * q + 16]))
    need("Y", t_d2)
    for k in range(8):
        t_e2 = dma("d_e2", Y.dma_start(out=T.e2[16 * k:16 * k + 16, :], in_=T.d2[:, :]))
    need("Y", t_i)
    for k in range(8):
        t_ec = dma("d_ec", Y.dma_start(out=T.ec[16 * k:16 * k + 16, :], in_=T.cr[0:96, :]))

    free = {}
    full = {}

    def product(i, bank, rhs, plane, n):
        if bank in free: need("P", free[bank])
        return p(P.matmul_mx(T.ps[:, 512 * bank:512 * bank + n], T.w1q[:, 128 * i:128 * i + 128], T.w1p[:, 128 * i:128 * i + 128], rhs, plane, True, True))

    def evacuate(i, bank, c0, n, tok):
        src, dst = T.ps[:, 512 * bank:512 * bank + n], R[i][:, c0:c0 + n]
        if i % 2 == 0:
            need("V", tok)
            full[i] = free[bank] = v(V.tensor_scalar(out=dst, in0=src, scalar1=0.0, scalar2=0.05, op0=MAX, op1=MULT))
        else:
            need("S", tok)
            full[i] = free[bank] = s(S.activation(out=dst, in_=src, func=RELU, scale=0.05))

    need("P", t_wq, t_xq)
    toks = [product(i, i, T.xq[:, :], T.xp[:, :], NODES) for i in range(4)]
    for i in range(4):
        evacuate(i, i, 0, NODES, toks[i])
    need("V", t_e1)
    t_o1 = v(V.tensor_copy(out=T.o1[:, :], in_=T.e1[:, :]))
    for a, sd in enumerate(arrive):
        k = slot(sd, r)
        es = near_eng if sd in near else far_eng
        need("P", ("a1_%d" % k, 2 * len(es)))
        b0 = 0 if a == 1 else 4
        toks = [product(i, b0 + i, T.c1[:, C1 * k:C1 * k + C1], T.p1[:, C1 * k:C1 * k + C1], C1) for i in range(4)]
        for i in range(4):
            evacuate(i, b0 + i, NODES + C1 * sd, C1, toks[i])

    def own(i, e, c0=0, c1=32): return R[i][:, 0:W1T].indirect(T.o1[:, 32 * e + c0:32 * e + c1])
    def cmp(i, e): return R[i][:, 0:W1T].indirect(T.oc[:, 12 * e:12 * e + 12])

    need("V", full[0], t_r)
    need("S", full[0], t_r, t_o1)
    need("V", t_o1)
    t_v = v(V.tensor_copy(out=T.h[:, 0:1024:4], in_=own(0, 0, 0, 16)))
    t_s = s(S.activation(out=T.h[:, 1024:2048:4], in_=own(0, 0, 16, 32), func=COPY))
    need("S", full[1], full[2], full[3])
    t_h1 = s(S.activation(out=T.h[:, 1:2048:4], in_=own(1, 0), func=COPY))
    for e in range(2):
        s(S.activation(out=T.bh[:, e:1536:3], in_=own(2, e), func=COPY))
    tok = t_v
    need("V", t_s)
    for e in (1, 2, 3):
        need("V", tok)
        tok = v(V.tensor_tensor(out=T.h[:, 0:2048:4], in0=own(0, e), in1=T.h[:, 0:2048:4], op=MAX))
    hdone = [tok]
    need("V", t_ec)
    for e in range(4):
        t_oc = v(V.tensor_copy(out=T.oc[:, 12 * e:12 * e + 12], in_=T.ec[:, e:48:4]))
    need("S", t_oc)
    t_b = {}
    for i in (1, 2, 3, 0):
        for e in range(3):
            t_b[i] = s(S.activation(out=T.bs[:, 576 * i + e:576 * i + 576:3], in_=cmp(i, e), func=COPY))
    need("V", full[1], full[2], full[3])
    tok = t_h1
    for e in (1, 2, 3):
        need("V", tok)
        tok = v(V.tensor_tensor(out=T.h[:, 1:2048:4], in0=own(1, e), in1=T.h[:, 1:2048:4], op=MAX))
    hdone.append(tok)
    need("V", t_mask, t_oc)

    def scan_l(i):
        need("V", t_b[i])
        return v(V.tensor_tensor_scan(T.bt[:, 576 * i:576 * i + 576], T.mask[:, 0:576], T.bs[:, 576 * i:576 * i + 576], 0.0, MULT, MAX))

    def last_l(i, tok):
        need("V", tok)
        return v(V.tensor_tensor(out=T.hs[:, i:768:4], in0=cmp(i, 3), in1=T.bt[:, 576 * i + 2:576 * i + 576:3], op=MAX))
    ta = scan_l(1)
    tb = scan_l(2)
    last_l(1, ta)
    last_l(2, tb)
    ta = scan_l(3)
    tb = scan_l(0)
    last_l(3, ta)
    tok = last_l(0, tb)
    need("V", tok)
    t_hs = v(V.quantize_mx(out=T.hsq[:, :], scales=T.hsp[:, :], in_=T.hs[:, :]))

    need("g", t_hs)
    engs = {far[0]: far_eng[:half], far[1]: far_eng[half:], near[0]: near_eng}
    cols = lambda a, k: a[:, C2 * k:C2 * k + C2]
    fused([(cols(T.c2, slot(r, d)).bitcast(U8), cols(T.hsq, slot(d, r)).bitcast(U8), d) for d in order], ["a2"] * 3, [engs[d] for d in order])
    fused([(cols(T.p2, slot(r, d)), cols(T.hsp, slot(d, r)), d) for d in order], ["a2"] * 3, [engs[d] for d in order])
    t_a2 = ("a2", 2 * (half + (len(far_eng) - half) + len(near_eng)))

    t_bh = {}
    t_bh[2] = s(S.activation(out=T.bh[:, 2:1536:3], in_=own(2, 2), func=COPY))
    for e in range(3):
        t_bh[3] = s(S.activation(out=T.bh[:, 1536 + e:3072:3], in_=own(3, e), func=COPY))
    need("V", t_e2)
    t_o2 = v(V.tensor_copy(out=T.o2[:, :], in_=T.e2[:, :]))
    for i in (2, 3):
        b0 = 1536 * (i - 2)
        need("V", t_bh[i])
        tok = v(V.tensor_tensor_scan(T.bi[:, b0:b0 + 1536], T.mask[:, :], T.bh[:, b0:b0 + 1536], 0.0, MULT, MAX))
        need("V", tok)
        hdone.append(v(V.tensor_tensor(out=T.h[:, i:2048:4], in0=own(i, 3), in1=T.bi[:, b0 + 2:b0 + 1536:3], op=MAX)))

    need("V", *hdone)
    t_hq = [v(V.quantize_mx(out=T.hq[:, 256 * k:256 * k + 256], scales=T.hp[:, 256 * k:256 * k + 256], in_=T.h[:, 1024 * k:1024 * k + 1024])) for k in range(2)]

    def product2(bank, rhs, plane, n):
        need("P", free[bank])
        return p(P.matmul_mx(T.ps[:, 512 * bank:512 * bank + n], T.w2q[:, :], T.w2p[:, :], rhs, plane, True, True))
    need("P", t_w2q)
    tu = []
    for k in range(2):
        need("P", t_hq[k])
        tu.append(product2(k, T.hq[:, 256 * k:256 * k + 256], T.hp[:, 256 * k:256 * k + 256], 256))
    need("P", t_a2)
    tu.append(product2(2, T.c2[:, :], T.p2[:, :], 3 * C2))
    need("S", tu[0])
    t_s = s(S.activation(out=T.u[:, 0:256], in_=T.ps[:, 0:256], func=COPY))
    need("V", tu[1])
    t_v = v(V.tensor_copy(out=T.u[:, 256:512], in_=T.ps[:, 512:768]))
    need("S", tu[2])
    for d, n in runs:
        k = slot(d, r)
        t_s = s(S.activation(out=T.u[:, NODES + C2 * d:NODES + C2 * (d + n)], in_=T.ps[:, 1024 + C2 * k:1024 + C2 * (k + n)], func=COPY))

    def tgt(e, c0=0, c1=16): return T.u[:, 0:W2T].indirect(T.o2[:, 16 * e + c0:16 * e + c1])
    need("V", t_u, t_o2, t_s, t_v)
    need("S", t_u, t_o2, t_s, t_v)
    tok = v(V.tensor_copy(out=T.yb[:, 0:128], in_=tgt(0, 0, 8)))
    t_s = s(S.activation(out=T.yb[:, 128:256], in_=tgt(0, 8, 16), func=COPY))
    need("V", t_s)
    for e in (1, 2, 3):
        need("V", tok)
        tok = v(V.tensor_tensor(out=T.yb[:, :], in0=tgt(e), in1=T.yb[:, :], op=MAX))
    need("Y", tok)
    t_y = dma("d_y", Y.dma_start(out=T.y[:, :], in_=T.yb[:, :]))

    need("g", ("sent", count["sent"]))
    need("Y", t_y, *[(k, count[k]) for k in ("cv", "cs", "ct")])
